import numpy as np
import ml_dtypes


def mxq(x, axis, fmt="e4m3"):
    dtype, down = {"e4m3": (ml_dtypes.float8_e4m3fn, 7), "e5m2": (ml_dtypes.float8_e5m2, 14)}[fmt]
    v = np.moveaxis(np.asarray(x, np.float32).astype(ml_dtypes.bfloat16).astype(np.float64), axis, -1)
    blocks = v.reshape(v.shape[:-1] + (-1, 32))
    amax = np.abs(blocks).max(-1, keepdims=True)
    byte = np.maximum(np.where(amax > 0, np.frexp(amax)[1] - 1 + 127, 0) - down, 1)
    scale = np.exp2(byte - 127.0)
    codes = (blocks / scale).astype(np.float32).astype(dtype).astype(np.float64)
    return np.moveaxis((codes * scale).reshape(v.shape), -1, axis)


WIDE = False


def mx_kscale(k):
    if not WIDE:
        return np.ones(k)
    levels = np.array([10, -10, 5, -5, 0])
    if k % 512:
        return np.exp2(np.random.permutation(np.resize(levels, k // 32))).repeat(32)
    a = np.empty((k // 512, 16))
    for p in range(k // 512):
        a[p, :8] = np.random.permutation(np.resize(levels, 8))
        for g in range(8):
            far = levels[np.abs(levels - a[p, g]) >= 10]
            a[p, g + 8] = far[np.random.randint(len(far))]
    return np.exp2(a.ravel()).repeat(32)


def f64(x):
    return np.asarray(x).astype(np.float64)


def striped(idx):
    return np.tile(idx.reshape(-1, 16).T, (8, 1)).astype(np.uint16)


def unstriped(offs):
    return offs[:16].T.reshape(-1).astype(np.int64)


def striped8(idx):
    return np.concatenate([x.reshape(-1, 16).T for x in idx]).astype(np.uint16)


def runs(offs, k):
    lists = np.stack([offs[16 * r : 16 * r + 16].T.reshape(-1) for r in range(8)]).astype(np.int64)
    return lists[np.arange(k) % 512 // 64]


def pack_weight(w):
    k, n = w.shape
    w = f64(np.asarray(w, np.float32).astype(ml_dtypes.bfloat16)).reshape(k // 32, 32, n)
    amax = np.abs(w).max(1)
    byte = np.clip(np.where(amax > 0, np.frexp(amax)[1] - 1 + 127 - 7, 1), 1, 254)
    scaled = (w * np.exp2(127.0 - byte)[:, None, :]).reshape(k, n).astype(np.float32)
    words = np.ascontiguousarray(scaled.reshape(k // 512, 128, 4, n).transpose(0, 1, 3, 2)).astype(ml_dtypes.float8_e4m3fn).view(np.uint8)
    return words, np.ascontiguousarray(byte.astype(np.uint8).reshape(k // 512, 16, n))


def unpack_weight(words, scales):
    g, p, n, _ = words.shape
    vals = np.ascontiguousarray(words).view(ml_dtypes.float8_e4m3fn).astype(np.float64) * np.repeat(np.exp2(scales.astype(np.float64) - 127.0), 8, axis=1)[..., None]
    return vals.transpose(0, 1, 3, 2).reshape(g * 512, n)


def sigmoid(v):
    return 1.0 / (1.0 + np.exp(-np.maximum(v, -700.0)))


K, T, S, N, G, H, W, U = 512, 1024, 512, 512, 2048, 512, 1024, 384


def setup_inputs():
    n = np.random.standard_normal
    s = mx_kscale(K)[:, None]
    u = mx_kscale(S)
    packed_xT = pack_weight(n((K, T)) * s)
    packed_dT = pack_weight(n((K, G)) / s)
    return {
        "x_words": packed_xT[0],
        "x_scales": packed_xT[1],
        "d_words": packed_dT[0],
        "d_scales": packed_dT[1],
        "gn": (np.random.uniform(0.5, 1.5, (H, 1)) * u[:, None]).astype(np.float32),
        "gm": (np.random.uniform(0.5, 1.5, (H, 1)) * u[:, None]).astype(np.float32),
        "w1": (n((H, N)) / np.sqrt(2 * H) / u[:, None]).astype(np.float32),
        "w2": (n((H, N)) / np.sqrt(2 * H) / u[:, None]).astype(np.float32),
        "offs": striped(np.random.permutation(T)[:S]),
        "k1": striped8(np.random.randint(0, G, (8, H))),
        "two": striped(np.random.permutation(T)[:S]),
        "k2": striped8(np.random.randint(0, G, (8, H))),
        "n1": striped8(np.stack([np.random.permutation(S) for _ in range(8)])),
        "n2": striped8(np.stack([np.random.permutation(S) for _ in range(8)])),
        "n3": striped(np.random.randint(0, S, W)),
        "n4": striped(np.random.permutation(S)[:U]),
        "n5": striped(np.random.permutation(S)[:U]),
    }


def reference(x_words, x_scales, d_words, d_scales, gn, gm, w1, w2, offs, k1, two, k2, n1, n2, n3, n4, n5):
    d_k1 = unpack_weight(d_words, d_scales)[np.arange(K)[:, None], runs(k1, K)]
    xq = unpack_weight(x_words, x_scales)[:, unstriped(offs)]
    a = 0.0625 * (d_k1.T @ xq)
    ex = np.exp(0.5 * a)
    z = f64(gn) * ((2.0 * ex) / (ex + ex[np.arange(H)[:, None], runs(n1, H)] + ex[np.arange(H)[:, None], runs(n2, H)]))
    d_k2 = unpack_weight(d_words, d_scales)[np.arange(K)[:, None], runs(k2, K)]
    x_two = unpack_weight(x_words, x_scales)[:, unstriped(two)]
    b = 0.0625 * (d_k2.T @ x_two)
    mb = b[:, unstriped(n3)]
    mn = mb.reshape(H, S, 2).min(axis=2)
    mx = mb.reshape(H, S, 2).max(axis=2)
    z2 = f64(gm) * ((b - mn) * sigmoid(mx))
    h = mxq(f64(w1), 0, "e4m3").T @ mxq(z, 0, "e4m3") + mxq(f64(w2), 0, "e4m3").T @ mxq(z2, 0, "e4m3")
    pa = h[:, unstriped(n5)]
    old = h[:, unstriped(n4)]
    ra = np.maximum(pa, 0.5 * old)
    out = h.copy()
    out[:, unstriped(n4)] = ra
    return out

@@ -1,0 +1,280 @@
+from contextlib import ExitStack
+
+import concourse.mybir as mybir
+
+K, T, S, N, G, H, W, U = 512, 1024, 512, 512, 2048, 512, 1024, 384
+FLOPS = 2 * K * H * S * 2 + 2 * H * N * S * 2
+
+F32 = mybir.dt.float32
+BF16 = mybir.dt.bfloat16
+U32 = mybir.dt.uint32
+I32 = mybir.dt.int32
+U16 = mybir.dt.uint16
+U8 = mybir.dt.uint8
+FP8X4 = mybir.dt.float8_e4m3fn_x4
+ALU = mybir.AluOpType
+ACT = mybir.ActivationFunctionType
+
+P = 128
+PACK = 4
+TILES = 4
+EX_WINDOW = 2 * S
+B_WINDOW = S + 32
+HALF = S // 2
+VECTOR_WEAVE = 160
+
+
+def tile_picked_pqjshareghardkmax_none_p_kernel(
+    tc, x_words, x_scales, d_words, d_scales, gn, gm, w1, w2, offs, k1, two, k2, n1, n2, n3, n4, n5, out
+):
+    nc = tc.nc
+    with ExitStack() as ctx:
+        keep = ctx.enter_context(tc.tile_pool(name="keep", bufs=1))
+        chain = ctx.enter_context(tc.tile_pool(name="chain", bufs=1))
+        psum = ctx.enter_context(tc.psum_pool(name="psum", bufs=1))
+
+        def load_list(name, src):
+            tile = keep.tile(list(src.shape), U16, name=name)
+            nc.sync.dma_start(tile[:], src)
+            return tile
+
+        d_bytes = keep.tile([P, G], U8, name="d_bytes")
+        x_bytes = keep.tile([P, T], U8, name="x_bytes")
+        nc.vector.memset(d_bytes[:].bitcast(I32), 0)
+        nc.gpsimd.memset(x_bytes[:].bitcast(I32), 0)
+        l_k1 = load_list("l_k1", k1)
+        l_offs = load_list("l_offs", offs)
+        x_table = keep.tile([P, T], U32, name="x_table")
+        d_table = keep.tile([P, G], U32, name="d_table")
+        nc.sync.dma_start(d_bytes[:].bitcast(I32)[0:P:8, :], d_scales[0].bitcast(I32))
+        nc.sync.dma_start(x_bytes[:].bitcast(I32)[0:P:8, :], x_scales[0].bitcast(I32))
+        nc.sync.dma_start(x_table[:].bitcast(I32), x_words[0].rearrange("p n t -> p (n t)").bitcast(I32))
+        nc.sync.dma_start(d_table[:].bitcast(I32), d_words[0].rearrange("p n t -> p (n t)").bitcast(I32))
+        l_k2 = load_list("l_k2", k2)
+        l_two = load_list("l_two", two)
+        l_n1 = load_list("l_n1", n1)
+        l_n2 = load_list("l_n2", n2)
+        l_n3 = load_list("l_n3", n3)
+        w1_raw = keep.tile([P, PACK, N], F32, name="w1_raw")
+        w2_raw = keep.tile([P, PACK, N], F32, name="w2_raw")
+        nc.sync.dma_start(w1_raw[:], w1.rearrange("(p j) m -> p j m", j=PACK))
+        nc.sync.dma_start(w2_raw[:], w2.rearrange("(p j) m -> p j m", j=PACK))
+        l_n4 = load_list("l_n4", n4)
+        l_n5 = load_list("l_n5", n5)
+
+        def coded_product(name, l_k, l_x, queue, k_bytes, x_picked_bytes, banks):
+            staged = keep.tile([P, H + S], U8, name=name + "_staged")
+            planes = keep.tile([P, H + S], U8, name=name + "_planes", align_bytes=64)
+            nc.vector.memset(planes[:].bitcast(I32), 0)
+            nc.vector.tensor_copy(k_bytes[:], d_bytes[:].indirect(l_k[:]))
+            nc.vector.tensor_copy(
+                staged[:, 0:H].rearrange("p (t m) -> p t m", t=PACK), k_bytes[:].rearrange("p (m t) -> p t m", t=PACK)
+            )
+            nc.vector.tensor_copy(x_picked_bytes[:], x_bytes[:].indirect(l_x[:]))
+            nc.vector.tensor_copy(staged[:].bitcast(I32)[:, H // 4 :], x_picked_bytes[:].bitcast(I32))
+            for r in range(4):
+                queue.dma_start(planes[:].bitcast(I32)[r:P:32, :], staged[:].bitcast(I32)[8 * r : P : 32, :])
+            x_codes = chain.tile([P, S], U32, name=name + "_x_codes", offset=4 * H, align_bytes=64)
+            nc.vector.tensor_copy(x_codes[:], x_table[:].indirect(l_x[:]))
+            k_words = chain.tile([P, H], U32, name=name + "_k_words", offset=0)
+            nc.vector.tensor_copy(k_words[:], d_table[:].indirect(l_k[:]))
+            k_codes = keep.tile([P, H], U32, name=name + "_k_codes", align_bytes=64)
+            nc.vector.tensor_copy(
+                k_codes[:].rearrange("p (t m) -> p t m", t=PACK), k_words[:].rearrange("p (m t) -> p t m", t=PACK)
+            )
+            sums = []
+            for t in range(TILES):
+                bank = psum.tile([P, S], F32, name=name + "_sum%d" % t, tag="bank%d" % (banks + t))
+                cols = slice(t * P, (t + 1) * P)
+                nc.tensor.matmul_mx(
+                    out=bank[:],
+                    lhsT=k_codes[:, cols].bitcast(FP8X4),
+                    lhsT_scale=planes[:, cols],
+                    rhs=x_codes[:].bitcast(FP8X4),
+                    rhs_scale=planes[:, H:],
+                    start=True,
+                    stop=True,
+                )
+                sums.append(bank)
+            return sums
+
+        def weave_views(grouped, rows, cols=slice(0, S)):
+            return (
+                grouped[:, cols, :].rearrange("p (c i) t -> p c t i", i=4),
+                rows[:, :, cols].rearrange("p t (c i) -> p c t i", i=4),
+            )
+
+        def round_weights(grouped, raw):
+            for q in range(4):
+                cols = slice(q * P, (q + 1) * P)
+                nc.gpsimd.tensor_scalar(
+                    grouped[:, cols, :], raw[:, :, cols].rearrange("p j m -> p m j"), 1.0, 0.0, ALU.mult, ALU.add
+                )
+
+        def quantize(name, grouped):
+            codes = keep.tile([P, S], U32, name=name + "_codes", align_bytes=64)
+            scales = keep.tile([P, S], U8, name=name + "_scales", align_bytes=64)
+            nc.vector.quantize_mx(
+                out=codes[:].bitcast(FP8X4), scales=scales[:], in_=grouped[:].rearrange("p w j -> p (w j)")
+            )
+            return codes, scales
+
+        a_k_bytes = chain.tile([P, H], U8, name="a_k_bytes", offset=4 * H)
+        a_x_bytes = chain.tile([P, S], U8, name="a_x_bytes", offset=8 * H)
+        a_sums = coded_product("a", l_k1, l_offs, nc.scalar, a_k_bytes, a_x_bytes, 0)
+
+        gn_t = chain.tile([P, PACK], F32, name="gn_t", offset=8 * H)
+        gm_t = chain.tile([P, PACK], F32, name="gm_t", offset=8 * H + 64)
+        nc.sync.dma_start(gn_t[:], gn.rearrange("(p t) o -> p (t o)", t=PACK))
+        nc.sync.dma_start(gm_t[:], gm.rearrange("(p t) o -> p (t o)", t=PACK))
+
+        w1_grouped = keep.tile([P, N, PACK], BF16, name="w1_grouped", align_bytes=64)
+        dst, src = weave_views(w1_grouped, w1_raw)
+        nc.scalar.copy(dst, src)
+
+        b_k_bytes = chain.tile([P, H], U8, name="b_k_bytes", offset=0)
+        b_x_bytes = chain.tile([P, S], U8, name="b_x_bytes", offset=H)
+        b_sums = coded_product("b", l_k2, l_two, nc.sync, b_k_bytes, b_x_bytes, TILES)
+
+        ex = [keep.tile([P, EX_WINDOW], F32, name="ex%d" % t) for t in range(TILES)]
+        for t in range(TILES):
+            nc.scalar.activation(ex[t][:, 0:S], a_sums[t][:], ACT.Exp, scale=0.03125)
+        first = keep.tile([P, TILES, S], F32, name="first")
+        both = keep.tile([P, TILES, S], F32, name="both")
+        for t in range(TILES):
+            nc.scalar.activation(first[:, t, :], ex[t][:].indirect(l_n1[:]), ACT.Copy)
+        for t in range(TILES):
+            nc.vector.tensor_tensor(both[:, t, :], ex[t][:].indirect(l_n2[:]), first[:, t, :], ALU.add)
+
+        b = [keep.tile([P, B_WINDOW], F32, name="b%d" % t) for t in range(TILES)]
+        members = keep.tile([P, TILES, S, 2], F32, name="members")
+        low = keep.tile([P, TILES, S], F32, name="low")
+        high = keep.tile([P, TILES, S], F32, name="high")
+        rise = keep.tile([P, TILES, S], F32, name="rise")
+        logs = first
+        gate = both
+        z_rows = keep.tile([P, TILES, S], BF16, name="z_rows")
+        z2_rows = keep.tile([P, TILES, S], BF16, name="z2_rows")
+        halves = (slice(0, HALF), slice(HALF, S))
+        pairs = ((0, 1), (2, 3))
+
+        def move(on_scalar, dst, src):
+            if on_scalar:
+                nc.scalar.activation(dst, src, ACT.Copy)
+            else:
+                nc.vector.tensor_copy(dst, src)
+
+        def fetch_members(half, t, on_scalar):
+            entries = l_n3[:, half * 32 : (half + 1) * 32]
+            move(on_scalar, members[:, t, halves[half], :].rearrange("p j e -> p (j e)"), b[t][:].indirect(entries))
+
+        def compare_members(half, pair):
+            cols = halves[half]
+            ts = slice(pair[0], pair[1] + 1)
+            nc.vector.tensor_tensor(high[:, ts, cols], members[:, ts, cols, 0], members[:, ts, cols, 1], ALU.max)
+            nc.vector.tensor_tensor(low[:, ts, cols], members[:, ts, cols, 0], members[:, ts, cols, 1], ALU.min)
+            nc.scalar.activation(gate[:, ts, cols], high[:, ts, cols], ACT.Sigmoid)
+            for t in pair:
+                nc.vector.tensor_tensor(rise[:, t, cols], b[t][:, cols], low[:, t, cols], ALU.subtract)
+
+        def gated(half, pair):
+            cols = halves[half]
+            for t in pair:
+                nc.vector.scalar_tensor_tensor(
+                    z2_rows[:, t, cols], rise[:, t, cols], gm_t[:, t : t + 1], gate[:, t, cols], ALU.mult, ALU.mult
+                )
+
+        for t in range(TILES):
+            nc.scalar.activation(b[t][:, 0:S], b_sums[t][:], ACT.Copy, scale=0.0625)
+        fetch_members(0, 0, True)
+        nc.scalar.activation(logs[:], both[:], ACT.Ln)
+        fetch_members(0, 1, False)
+        fetch_members(0, 2, False)
+
+        w1_codes, w1_scales = quantize("w1", w1_grouped)
+        w2_grouped = keep.tile([P, N, PACK], BF16, name="w2_grouped", align_bytes=64)
+        dst, src = weave_views(w2_grouped, w2_raw)
+        nc.vector.tensor_copy(dst, src)
+        w2_codes, w2_scales = quantize("w2", w2_grouped)
+        logit = keep.tile([P, TILES, S], F32, name="logit")
+        share = keep.tile([P, TILES, S], F32, name="share")
+        for t in range(TILES):
+            nc.vector.scalar_tensor_tensor(logit[:, t, :], a_sums[t][:], 0.03125, logs[:, t, :], ALU.mult, ALU.subtract)
+        for t in range(TILES):
+            nc.scalar.activation(share[:, t, :], logit[:, t, :], ACT.Sigmoid)
+        for t in range(TILES):
+            nc.vector.tensor_scalar(z_rows[:, t, :], share[:, t, :], gn_t[:, t : t + 1], 2.0, ALU.mult, ALU.mult)
+        z_grouped = keep.tile([P, S, PACK], BF16, name="z_grouped", align_bytes=64)
+        dst, src = weave_views(z_grouped, z_rows)
+        nc.vector.tensor_copy(dst, src)
+        z_codes, z_scales = quantize("z", z_grouped)
+
+        z2_grouped = keep.tile([P, S, PACK], BF16, name="z2_grouped", align_bytes=64)
+        z2_codes = keep.tile([P, S], U32, name="z2_codes", align_bytes=64)
+        z2_scales = keep.tile([P, S], U8, name="z2_scales", align_bytes=64)
+
+        def quantize_z2(half):
+            cols = halves[half]
+            nc.vector.quantize_mx(
+                out=z2_codes[:, cols].bitcast(FP8X4),
+                scales=z2_scales[:, cols],
+                in_=z2_grouped[:, cols, :].rearrange("p w j -> p (w j)"),
+            )
+
+        compare_members(0, pairs[0])
+        fetch_members(0, 3, True)
+        compare_members(0, pairs[1])
+        gated(0, pairs[0])
+        fetch_members(1, 0, True)
+        fetch_members(1, 1, True)
+        compare_members(1, pairs[0])
+        gated(0, pairs[1])
+        dst, src = weave_views(z2_grouped, z2_rows, halves[0])
+        nc.scalar.copy(dst, src)
+        quantize_z2(0)
+        fetch_members(1, 2, True)
+        fetch_members(1, 3, True)
+        compare_members(1, pairs[1])
+        gated(1, pairs[0])
+        gated(1, pairs[1])
+        dst, src = weave_views(z2_grouped, z2_rows, slice(HALF, HALF + VECTOR_WEAVE))
+        nc.vector.tensor_copy(dst, src)
+        dst, src = weave_views(z2_grouped, z2_rows, slice(HALF + VECTOR_WEAVE, S))
+        nc.scalar.copy(dst, src)
+        quantize_z2(1)
+
+        h = [keep.tile([P, S], F32, name="h%d" % m) for m in range(TILES)]
+        for half in range(2):
+            cols = halves[half]
+            h_sums = [
+                psum.tile([P, HALF], F32, name="h_sum%d_%d" % (half, m), tag="bank%d" % ((1 - half) * TILES + m))
+                for m in range(TILES)
+            ]
+            for step, (w_codes, w_scales, v_codes, v_scales) in enumerate(
+                ((w1_codes, w1_scales, z_codes, z_scales), (w2_codes, w2_scales, z2_codes, z2_scales))
+            ):
+                for m in range(TILES):
+                    rows = slice(m * P, (m + 1) * P)
+                    nc.tensor.matmul_mx(
+                        out=h_sums[m][:],
+                        lhsT=w_codes[:, rows].bitcast(FP8X4),
+                        lhsT_scale=w_scales[:, rows],
+                        rhs=v_codes[:, cols].bitcast(FP8X4),
+                        rhs_scale=v_scales[:, cols],
+                        start=(step == 0),
+                        stop=(step == 1),
+                    )
+            for m in range(TILES):
+                move(half == 0 or m != 1, h[m][:, cols], h_sums[m][:])
+
+        pa = [keep.tile([P, U], F32, name="pa%d" % m) for m in range(TILES)]
+        old = [keep.tile([P, U], F32, name="old%d" % m) for m in range(TILES)]
+        ra = [keep.tile([P, U], F32, name="ra%d" % m) for m in range(TILES)]
+        for m in range(TILES):
+            move(m % 2 == 0, pa[m][:], h[m][:].indirect(l_n5[:]))
+            move(m != 1, old[m][:], h[m][:].indirect(l_n4[:]))
+        for m in range(TILES):
+            nc.vector.scalar_tensor_tensor(ra[m][:], old[m][:], 0.5, pa[m][:], ALU.mult, ALU.max)
+        for m in range(TILES):
+            move(m % 2 == 0, h[m][:].indirect(l_n4[:]), ra[m][:])
+            nc.sync.dma_start(out[m * P : (m + 1) * P, :], h[m][:])

@@ -40,8 +40,9 @@ def tile_picked_pqjshareghardkmax_none_p_kernel(
 
         d_bytes = keep.tile([P, G], U8, name="d_bytes")
         x_bytes = keep.tile([P, T], U8, name="x_bytes")
-        nc.vector.memset(d_bytes[:].bitcast(I32), 0)
-        nc.gpsimd.memset(x_bytes[:].bitcast(I32), 0)
+        nc.vector.memset(d_bytes[:].bitcast(I32)[:, 0 : G // 8], 0)
+        nc.gpsimd.memset(d_bytes[:].bitcast(I32)[:, G // 8 :], 0)
+        nc.vector.memset(x_bytes[:].bitcast(I32), 0)
         l_k1 = load_list("l_k1", k1)
         l_offs = load_list("l_offs", offs)
         x_table = keep.tile([P, T], U32, name="x_table")
@@ -55,10 +56,6 @@ def tile_picked_pqjshareghardkmax_none_p_kernel(
         l_n1 = load_list("l_n1", n1)
         l_n2 = load_list("l_n2", n2)
         l_n3 = load_list("l_n3", n3)
-        w1_raw = keep.tile([P, PACK, N], F32, name="w1_raw")
-        w2_raw = keep.tile([P, PACK, N], F32, name="w2_raw")
-        nc.sync.dma_start(w1_raw[:], w1.rearrange("(p j) m -> p j m", j=PACK))
-        nc.sync.dma_start(w2_raw[:], w2.rearrange("(p j) m -> p j m", j=PACK))
         l_n4 = load_list("l_n4", n4)
         l_n5 = load_list("l_n5", n5)
 
@@ -119,18 +116,23 @@ def tile_picked_pqjshareghardkmax_none_p_kernel(
             )
             return codes, scales
 
-        a_k_bytes = chain.tile([P, H], U8, name="a_k_bytes", offset=4 * H)
-        a_x_bytes = chain.tile([P, S], U8, name="a_x_bytes", offset=8 * H)
+        a_k_bytes = chain.tile([P, H], U8, name="a_k_bytes", offset=40 * H)
+        a_x_bytes = chain.tile([P, S], U8, name="a_x_bytes", offset=24 * H - 256)
         a_sums = coded_product("a", l_k1, l_offs, nc.scalar, a_k_bytes, a_x_bytes, 0)
 
-        gn_t = chain.tile([P, PACK], F32, name="gn_t", offset=8 * H)
-        gm_t = chain.tile([P, PACK], F32, name="gm_t", offset=8 * H + 64)
+        w1_raw = chain.tile([P, PACK, N], F32, name="w1_raw", offset=8 * H)
+        w2_raw = chain.tile([P, PACK, N], F32, name="w2_raw", offset=24 * H)
+        nc.scalar.dma_start(w1_raw[:], w1.rearrange("(p j) m -> p j m", j=PACK))
+        nc.scalar.dma_start(w2_raw[:], w2.rearrange("(p j) m -> p j m", j=PACK))
+        gn_t = chain.tile([P, PACK], F32, name="gn_t", offset=40 * H)
+        gm_t = chain.tile([P, PACK], F32, name="gm_t", offset=40 * H + 64)
         nc.sync.dma_start(gn_t[:], gn.rearrange("(p t) o -> p (t o)", t=PACK))
         nc.sync.dma_start(gm_t[:], gm.rearrange("(p t) o -> p (t o)", t=PACK))
 
         w1_grouped = keep.tile([P, N, PACK], BF16, name="w1_grouped", align_bytes=64)
-        dst, src = weave_views(w1_grouped, w1_raw)
-        nc.scalar.copy(dst, src)
+        round_weights(w1_grouped, w1_raw)
+        w2_grouped = keep.tile([P, N, PACK], BF16, name="w2_grouped", align_bytes=64)
+        round_weights(w2_grouped, w2_raw)
 
         b_k_bytes = chain.tile([P, H], U8, name="b_k_bytes", offset=0)
         b_x_bytes = chain.tile([P, S], U8, name="b_x_bytes", offset=H)
@@ -192,9 +194,6 @@ def tile_picked_pqjshareghardkmax_none_p_kernel(
         fetch_members(0, 2, False)
 
         w1_codes, w1_scales = quantize("w1", w1_grouped)
-        w2_grouped = keep.tile([P, N, PACK], BF16, name="w2_grouped", align_bytes=64)
-        dst, src = weave_views(w2_grouped, w2_raw)
-        nc.vector.tensor_copy(dst, src)
         w2_codes, w2_scales = quantize("w2", w2_grouped)
         logit = keep.tile([P, TILES, S], F32, name="logit")
         share = keep.tile([P, TILES, S], F32, name="share")

@@ -50,12 +50,16 @@ def tile_picked_pqjshareghardkmax_none_p_kernel(
         nc.sync.dma_start(d_bytes[:].bitcast(I32)[0:P:8, :], d_scales[0].bitcast(I32))
         nc.sync.dma_start(x_bytes[:].bitcast(I32)[0:P:8, :], x_scales[0].bitcast(I32))
         nc.sync.dma_start(x_table[:].bitcast(I32), x_words[0].rearrange("p n t -> p (n t)").bitcast(I32))
-        nc.sync.dma_start(d_table[:].bitcast(I32), d_words[0].rearrange("p n t -> p (n t)").bitcast(I32))
+        w1_rows = w1.rearrange("(p j) m -> p j m", j=PACK)
+        w1_raw = [chain.tile([P, PACK, HALF], F32, name="w1_raw%d" % q, offset=(8 + 8 * q) * H) for q in range(2)]
+        nc.sync.dma_start(w1_raw[0][:], w1_rows[:, :, 0:HALF])
         l_k2 = load_list("l_k2", k2)
         l_two = load_list("l_two", two)
         l_n1 = load_list("l_n1", n1)
         l_n2 = load_list("l_n2", n2)
         l_n3 = load_list("l_n3", n3)
+        nc.sync.dma_start(d_table[:].bitcast(I32), d_words[0].rearrange("p n t -> p (n t)").bitcast(I32))
+        nc.sync.dma_start(w1_raw[1][:], w1_rows[:, :, HALF:])
         l_n4 = load_list("l_n4", n4)
         l_n5 = load_list("l_n5", n5)
 
@@ -117,28 +121,29 @@ def tile_picked_pqjshareghardkmax_none_p_kernel(
             return codes, scales
 
         a_k_bytes = chain.tile([P, H], U8, name="a_k_bytes", offset=40 * H)
-        a_x_bytes = chain.tile([P, S], U8, name="a_x_bytes", offset=24 * H - 256)
-        a_sums = coded_product("a", l_k1, l_offs, nc.scalar, a_k_bytes, a_x_bytes, 0)
+        a_x_bytes = chain.tile([P, S], U8, name="a_x_bytes", offset=24 * H)
+        a_sums = coded_product("a", l_k1, l_offs, nc.sync, a_k_bytes, a_x_bytes, 0)
 
-        w1_raw = chain.tile([P, PACK, N], F32, name="w1_raw", offset=8 * H)
         w2_raw = chain.tile([P, PACK, N], F32, name="w2_raw", offset=24 * H)
-        nc.scalar.dma_start(w1_raw[:], w1.rearrange("(p j) m -> p j m", j=PACK))
-        nc.scalar.dma_start(w2_raw[:], w2.rearrange("(p j) m -> p j m", j=PACK))
+        nc.sync.dma_start(w2_raw[:], w2.rearrange("(p j) m -> p j m", j=PACK))
         gn_t = chain.tile([P, PACK], F32, name="gn_t", offset=40 * H)
         gm_t = chain.tile([P, PACK], F32, name="gm_t", offset=40 * H + 64)
         nc.sync.dma_start(gn_t[:], gn.rearrange("(p t) o -> p (t o)", t=PACK))
         nc.sync.dma_start(gm_t[:], gm.rearrange("(p t) o -> p (t o)", t=PACK))
 
         w1_grouped = keep.tile([P, N, PACK], BF16, name="w1_grouped", align_bytes=64)
-        round_weights(w1_grouped, w1_raw)
-        w2_grouped = keep.tile([P, N, PACK], BF16, name="w2_grouped", align_bytes=64)
-        round_weights(w2_grouped, w2_raw)
+        for q in range(2):
+            nc.scalar.copy(
+                w1_grouped[:, q * HALF : (q + 1) * HALF, :].rearrange("p (c i) t -> p c t i", i=4),
+                w1_raw[q][:].rearrange("p t (c i) -> p c t i", i=4),
+            )
 
         b_k_bytes = chain.tile([P, H], U8, name="b_k_bytes", offset=0)
         b_x_bytes = chain.tile([P, S], U8, name="b_x_bytes", offset=H)
         b_sums = coded_product("b", l_k2, l_two, nc.sync, b_k_bytes, b_x_bytes, TILES)
 
-        ex = [keep.tile([P, EX_WINDOW], F32, name="ex%d" % t) for t in range(TILES)]
+        ex = [chain.tile([P, EX_WINDOW], F32, name="ex%d" % t, offset=(16 - 8 * t) * H) for t in range(2)]
+        ex = ex + [keep.tile([P, EX_WINDOW], F32, name="ex%d" % t) for t in range(2, TILES)]
         for t in range(TILES):
             nc.scalar.activation(ex[t][:, 0:S], a_sums[t][:], ACT.Exp, scale=0.03125)
         first = keep.tile([P, TILES, S], F32, name="first")
@@ -194,6 +199,9 @@ def tile_picked_pqjshareghardkmax_none_p_kernel(
         fetch_members(0, 2, False)
 
         w1_codes, w1_scales = quantize("w1", w1_grouped)
+        w2_grouped = chain.tile([P, N, PACK], BF16, name="w2_grouped", offset=8 * H, align_bytes=64)
+        dst, src = weave_views(w2_grouped, w2_raw)
+        nc.vector.tensor_copy(dst, src)
         w2_codes, w2_scales = quantize("w2", w2_grouped)
         logit = keep.tile([P, TILES, S], F32, name="logit")
         share = keep.tile([P, TILES, S], F32, name="share")

@@ -51,20 +51,19 @@ def tile_picked_pqjshareghardkmax_none_p_kernel(
         nc.sync.dma_start(x_bytes[:].bitcast(I32)[0:P:8, :], x_scales[0].bitcast(I32))
         nc.sync.dma_start(x_table[:].bitcast(I32), x_words[0].rearrange("p n t -> p (n t)").bitcast(I32))
         w1_rows = w1.rearrange("(p j) m -> p j m", j=PACK)
-        w1_raw = [chain.tile([P, PACK, HALF], F32, name="w1_raw%d" % q, offset=(8 + 8 * q) * H) for q in range(2)]
-        nc.sync.dma_start(w1_raw[0][:], w1_rows[:, :, 0:HALF])
+        w1_raw = [chain.tile([P, PACK, HALF], F32, name="w1_raw%d" % q, offset=(13 + 8 * q) * H) for q in range(2)]
+        nc.sync.dma_start(d_table[:].bitcast(I32), d_words[0].rearrange("p n t -> p (n t)").bitcast(I32))
         l_k2 = load_list("l_k2", k2)
         l_two = load_list("l_two", two)
         l_n1 = load_list("l_n1", n1)
         l_n2 = load_list("l_n2", n2)
         l_n3 = load_list("l_n3", n3)
-        nc.sync.dma_start(d_table[:].bitcast(I32), d_words[0].rearrange("p n t -> p (n t)").bitcast(I32))
+        nc.sync.dma_start(w1_raw[0][:], w1_rows[:, :, 0:HALF])
         nc.sync.dma_start(w1_raw[1][:], w1_rows[:, :, HALF:])
         l_n4 = load_list("l_n4", n4)
         l_n5 = load_list("l_n5", n5)
 
-        def coded_product(name, l_k, l_x, queue, k_bytes, x_picked_bytes, banks):
-            staged = keep.tile([P, H + S], U8, name=name + "_staged")
+        def coded_product(name, l_k, l_x, queue, k_bytes, x_picked_bytes, staged, words_at, banks):
             planes = keep.tile([P, H + S], U8, name=name + "_planes", align_bytes=64)
             nc.vector.memset(planes[:].bitcast(I32), 0)
             nc.vector.tensor_copy(k_bytes[:], d_bytes[:].indirect(l_k[:]))
@@ -75,13 +74,13 @@ def tile_picked_pqjshareghardkmax_none_p_kernel(
             nc.vector.tensor_copy(staged[:].bitcast(I32)[:, H // 4 :], x_picked_bytes[:].bitcast(I32))
             for r in range(4):
                 queue.dma_start(planes[:].bitcast(I32)[r:P:32, :], staged[:].bitcast(I32)[8 * r : P : 32, :])
-            x_codes = chain.tile([P, S], U32, name=name + "_x_codes", offset=4 * H, align_bytes=64)
+            x_codes = chain.tile([P, S], U32, name=name + "_x_codes", offset=8 * H, align_bytes=64)
             nc.vector.tensor_copy(x_codes[:], x_table[:].indirect(l_x[:]))
-            k_words = chain.tile([P, H], U32, name=name + "_k_words", offset=0)
+            k_words = chain.tile([P, H], U32, name=name + "_k_words", offset=words_at)
             nc.vector.tensor_copy(k_words[:], d_table[:].indirect(l_k[:]))
             k_codes = keep.tile([P, H], U32, name=name + "_k_codes", align_bytes=64)
             nc.vector.tensor_copy(
-                k_codes[:].rearrange("p (t m) -> p t m", t=PACK), k_words[:].rearrange("p (m t) -> p t m", t=PACK)
+                k_codes[:].rearrange("p (t m) -> p m t", t=PACK), k_words[:].rearrange("p (m t) -> p m t", t=PACK)
             )
             sums = []
             for t in range(TILES):
@@ -120,14 +119,15 @@ def tile_picked_pqjshareghardkmax_none_p_kernel(
             )
             return codes, scales
 
-        a_k_bytes = chain.tile([P, H], U8, name="a_k_bytes", offset=40 * H)
-        a_x_bytes = chain.tile([P, S], U8, name="a_x_bytes", offset=24 * H)
-        a_sums = coded_product("a", l_k1, l_offs, nc.sync, a_k_bytes, a_x_bytes, 0)
+        a_k_bytes = chain.tile([P, H], U8, name="a_k_bytes", offset=12 * H)
+        a_x_bytes = chain.tile([P, S], U8, name="a_x_bytes", offset=29 * H)
+        a_staged = keep.tile([P, H + S], U8, name="a_staged")
+        a_sums = coded_product("a", l_k1, l_offs, nc.sync, a_k_bytes, a_x_bytes, a_staged, 4 * H, 0)
 
-        w2_raw = chain.tile([P, PACK, N], F32, name="w2_raw", offset=24 * H)
+        w2_raw = chain.tile([P, PACK, N], F32, name="w2_raw", offset=29 * H + 256)
         nc.sync.dma_start(w2_raw[:], w2.rearrange("(p j) m -> p j m", j=PACK))
-        gn_t = chain.tile([P, PACK], F32, name="gn_t", offset=40 * H)
-        gm_t = chain.tile([P, PACK], F32, name="gm_t", offset=40 * H + 64)
+        gn_t = chain.tile([P, PACK], F32, name="gn_t", offset=29 * H)
+        gm_t = chain.tile([P, PACK], F32, name="gm_t", offset=29 * H + 64)
         nc.sync.dma_start(gn_t[:], gn.rearrange("(p t) o -> p (t o)", t=PACK))
         nc.sync.dma_start(gm_t[:], gm.rearrange("(p t) o -> p (t o)", t=PACK))
 
@@ -138,11 +138,12 @@ def tile_picked_pqjshareghardkmax_none_p_kernel(
                 w1_raw[q][:].rearrange("p t (c i) -> p c t i", i=4),
             )
 
-        b_k_bytes = chain.tile([P, H], U8, name="b_k_bytes", offset=0)
-        b_x_bytes = chain.tile([P, S], U8, name="b_x_bytes", offset=H)
-        b_sums = coded_product("b", l_k2, l_two, nc.sync, b_k_bytes, b_x_bytes, TILES)
+        b_k_bytes = chain.tile([P, H], U8, name="b_k_bytes", offset=5 * H)
+        b_x_bytes = chain.tile([P, S], U8, name="b_x_bytes", offset=7 * H)
+        b_staged = keep.tile([P, H + S], U8, name="b_staged")
+        b_sums = coded_product("b", l_k2, l_two, nc.sync, b_k_bytes, b_x_bytes, b_staged, H, TILES)
 
-        ex = [chain.tile([P, EX_WINDOW], F32, name="ex%d" % t, offset=(16 - 8 * t) * H) for t in range(2)]
+        ex = [chain.tile([P, EX_WINDOW], F32, name="ex%d" % t, offset=(21 - 8 * t) * H) for t in range(2)]
         ex = ex + [keep.tile([P, EX_WINDOW], F32, name="ex%d" % t) for t in range(2, TILES)]
         for t in range(TILES):
             nc.scalar.activation(ex[t][:, 0:S], a_sums[t][:], ACT.Exp, scale=0.03125)
@@ -160,7 +161,8 @@ def tile_picked_pqjshareghardkmax_none_p_kernel(
         rise = keep.tile([P, TILES, S], F32, name="rise")
         logs = first
         gate = both
-        z_rows = keep.tile([P, TILES, S], BF16, name="z_rows")
+        gn_twice = keep.tile([P, PACK], F32, name="gn_twice")
+        nc.vector.tensor_scalar(gn_twice[:], gn_t[:], 2.0, None, ALU.mult)
         z2_rows = keep.tile([P, TILES, S], BF16, name="z2_rows")
         halves = (slice(0, HALF), slice(HALF, S))
         pairs = ((0, 1), (2, 3))
@@ -199,7 +201,7 @@ def tile_picked_pqjshareghardkmax_none_p_kernel(
         fetch_members(0, 2, False)
 
         w1_codes, w1_scales = quantize("w1", w1_grouped)
-        w2_grouped = chain.tile([P, N, PACK], BF16, name="w2_grouped", offset=8 * H, align_bytes=64)
+        w2_grouped = chain.tile([P, N, PACK], BF16, name="w2_grouped", offset=13 * H, align_bytes=64)
         dst, src = weave_views(w2_grouped, w2_raw)
         nc.vector.tensor_copy(dst, src)
         w2_codes, w2_scales = quantize("w2", w2_grouped)
@@ -209,11 +211,10 @@ def tile_picked_pqjshareghardkmax_none_p_kernel(
             nc.vector.scalar_tensor_tensor(logit[:, t, :], a_sums[t][:], 0.03125, logs[:, t, :], ALU.mult, ALU.subtract)
         for t in range(TILES):
             nc.scalar.activation(share[:, t, :], logit[:, t, :], ACT.Sigmoid)
-        for t in range(TILES):
-            nc.vector.tensor_scalar(z_rows[:, t, :], share[:, t, :], gn_t[:, t : t + 1], 2.0, ALU.mult, ALU.mult)
         z_grouped = keep.tile([P, S, PACK], BF16, name="z_grouped", align_bytes=64)
-        dst, src = weave_views(z_grouped, z_rows)
-        nc.vector.tensor_copy(dst, src)
+        dst, src = weave_views(z_grouped, share)
+        gains = gn_twice[:].unsqueeze(1).unsqueeze(3).to_broadcast([P, S // 4, PACK, 4])
+        nc.vector.tensor_tensor(dst, src, gains, ALU.mult)
         z_codes, z_scales = quantize("z", z_grouped)
 
         z2_grouped = keep.tile([P, S, PACK], BF16, name="z2_grouped", align_bytes=64)
@@ -244,10 +245,8 @@ def tile_picked_pqjshareghardkmax_none_p_kernel(
         compare_members(1, pairs[1])
         gated(1, pairs[0])
         gated(1, pairs[1])
-        dst, src = weave_views(z2_grouped, z2_rows, slice(HALF, HALF + VECTOR_WEAVE))
+        dst, src = weave_views(z2_grouped, z2_rows, halves[1])
         nc.vector.tensor_copy(dst, src)
-        dst, src = weave_views(z2_grouped, z2_rows, slice(HALF + VECTOR_WEAVE, S))
-        nc.scalar.copy(dst, src)
         quantize_z2(1)
 
         h = [keep.tile([P, S], F32, name="h%d" % m) for m in range(TILES)]

from contextlib import ExitStack

import concourse.mybir as mybir

K, T, S, N, G, H, W, U = 512, 1024, 512, 512, 2048, 512, 1024, 384
FLOPS = 2 * K * H * S * 2 + 2 * H * N * S * 2

F32 = mybir.dt.float32
BF16 = mybir.dt.bfloat16
U32 = mybir.dt.uint32
I32 = mybir.dt.int32
U16 = mybir.dt.uint16
U8 = mybir.dt.uint8
FP8X4 = mybir.dt.float8_e4m3fn_x4
ALU = mybir.AluOpType
ACT = mybir.ActivationFunctionType

P = 128
PACK = 4
TILES = 4
EX_WINDOW = 2 * S
B_WINDOW = S + 32
HALF = S // 2
VECTOR_WEAVE = 160


def tile_picked_pqjshareghardkmax_none_p_kernel(
    tc, x_words, x_scales, d_words, d_scales, gn, gm, w1, w2, offs, k1, two, k2, n1, n2, n3, n4, n5, out
):
    nc = tc.nc
    with ExitStack() as ctx:
        keep = ctx.enter_context(tc.tile_pool(name="keep", bufs=1))
        chain = ctx.enter_context(tc.tile_pool(name="chain", bufs=1))
        psum = ctx.enter_context(tc.psum_pool(name="psum", bufs=1))

        def load_list(name, src):
            tile = keep.tile(list(src.shape), U16, name=name)
            nc.sync.dma_start(tile[:], src)
            return tile

        d_bytes = keep.tile([P, G], U8, name="d_bytes")
        x_bytes = keep.tile([P, T], U8, name="x_bytes")
        nc.vector.memset(d_bytes[:].bitcast(I32)[:, 0 : G // 8], 0)
        nc.gpsimd.memset(d_bytes[:].bitcast(I32)[:, G // 8 :], 0)
        nc.vector.memset(x_bytes[:].bitcast(I32), 0)
        l_k1 = load_list("l_k1", k1)
        l_offs = load_list("l_offs", offs)
        x_table = keep.tile([P, T], U32, name="x_table")
        d_table = keep.tile([P, G], U32, name="d_table")
        nc.sync.dma_start(d_bytes[:].bitcast(I32)[0:P:8, :], d_scales[0].bitcast(I32))
        nc.sync.dma_start(x_bytes[:].bitcast(I32)[0:P:8, :], x_scales[0].bitcast(I32))
        nc.sync.dma_start(x_table[:].bitcast(I32), x_words[0].rearrange("p n t -> p (n t)").bitcast(I32))
        w1_rows = w1.rearrange("(p j) m -> p j m", j=PACK)
        w1_raw = [chain.tile([P, PACK, HALF], F32, name="w1_raw%d" % q, offset=(13 + 8 * q) * H) for q in range(2)]
        nc.sync.dma_start(d_table[:].bitcast(I32), d_words[0].rearrange("p n t -> p (n t)").bitcast(I32))
        l_k2 = load_list("l_k2", k2)
        l_two = load_list("l_two", two)
        l_n1 = load_list("l_n1", n1)
        l_n2 = load_list("l_n2", n2)
        l_n3 = load_list("l_n3", n3)
        nc.sync.dma_start(w1_raw[0][:], w1_rows[:, :, 0:HALF])
        nc.sync.dma_start(w1_raw[1][:], w1_rows[:, :, HALF:])
        l_n4 = load_list("l_n4", n4)
        l_n5 = load_list("l_n5", n5)

        def coded_product(name, l_k, l_x, queue, k_bytes, x_picked_bytes, staged, words_at, banks):
            planes = keep.tile([P, H + S], U8, name=name + "_planes", align_bytes=64)
            nc.vector.memset(planes[:].bitcast(I32), 0)
            nc.vector.tensor_copy(k_bytes[:], d_bytes[:].indirect(l_k[:]))
            nc.vector.tensor_copy(
                staged[:, 0:H].rearrange("p (t m) -> p t m", t=PACK), k_bytes[:].rearrange("p (m t) -> p t m", t=PACK)
            )
            nc.vector.tensor_copy(x_picked_bytes[:], x_bytes[:].indirect(l_x[:]))
            nc.vector.tensor_copy(staged[:].bitcast(I32)[:, H // 4 :], x_picked_bytes[:].bitcast(I32))
            for r in range(4):
                queue.dma_start(planes[:].bitcast(I32)[r:P:32, :], staged[:].bitcast(I32)[8 * r : P : 32, :])
            x_codes = chain.tile([P, S], U32, name=name + "_x_codes", offset=8 * H, align_bytes=64)
            nc.vector.tensor_copy(x_codes[:], x_table[:].indirect(l_x[:]))
            k_words = chain.tile([P, H], U32, name=name + "_k_words", offset=words_at)
            nc.vector.tensor_copy(k_words[:], d_table[:].indirect(l_k[:]))
            k_codes = keep.tile([P, H], U32, name=name + "_k_codes", align_bytes=64)
            nc.vector.tensor_copy(
                k_codes[:].rearrange("p (t m) -> p m t", t=PACK), k_words[:].rearrange("p (m t) -> p m t", t=PACK)
            )
            sums = []
            for t in range(TILES):
                bank = psum.tile([P, S], F32, name=name + "_sum%d" % t, tag="bank%d" % (banks + t))
                cols = slice(t * P, (t + 1) * P)
                nc.tensor.matmul_mx(
                    out=bank[:],
                    lhsT=k_codes[:, cols].bitcast(FP8X4),
                    lhsT_scale=planes[:, cols],
                    rhs=x_codes[:].bitcast(FP8X4),
                    rhs_scale=planes[:, H:],
                    start=True,
                    stop=True,
                )
                sums.append(bank)
            return sums

        def weave_views(grouped, rows, cols=slice(0, S)):
            return (
                grouped[:, cols, :].rearrange("p (c i) t -> p c t i", i=4),
                rows[:, :, cols].rearrange("p t (c i) -> p c t i", i=4),
            )

        def round_weights(grouped, raw):
            for q in range(4):
                cols = slice(q * P, (q + 1) * P)
                nc.gpsimd.tensor_scalar(
                    grouped[:, cols, :], raw[:, :, cols].rearrange("p j m -> p m j"), 1.0, 0.0, ALU.mult, ALU.add
                )

        def quantize(name, grouped):
            codes = keep.tile([P, S], U32, name=name + "_codes", align_bytes=64)
            scales = keep.tile([P, S], U8, name=name + "_scales", align_bytes=64)
            nc.vector.quantize_mx(
                out=codes[:].bitcast(FP8X4), scales=scales[:], in_=grouped[:].rearrange("p w j -> p (w j)")
            )
            return codes, scales

        a_k_bytes = chain.tile([P, H], U8, name="a_k_bytes", offset=12 * H)
        a_x_bytes = chain.tile([P, S], U8, name="a_x_bytes", offset=29 * H)
        a_staged = keep.tile([P, H + S], U8, name="a_staged")
        a_sums = coded_product("a", l_k1, l_offs, nc.sync, a_k_bytes, a_x_bytes, a_staged, 4 * H, 0)

        w2_raw = chain.tile([P, PACK, N], F32, name="w2_raw", offset=29 * H + 256)
        nc.sync.dma_start(w2_raw[:], w2.rearrange("(p j) m -> p j m", j=PACK))
        gn_t = chain.tile([P, PACK], F32, name="gn_t", offset=29 * H)
        gm_t = chain.tile([P, PACK], F32, name="gm_t", offset=29 * H + 64)
        nc.sync.dma_start(gn_t[:], gn.rearrange("(p t) o -> p (t o)", t=PACK))
        nc.sync.dma_start(gm_t[:], gm.rearrange("(p t) o -> p (t o)", t=PACK))

        w1_grouped = keep.tile([P, N, PACK], BF16, name="w1_grouped", align_bytes=64)
        for q in range(2):
            nc.scalar.copy(
                w1_grouped[:, q * HALF : (q + 1) * HALF, :].rearrange("p (c i) t -> p c t i", i=4),
                w1_raw[q][:].rearrange("p t (c i) -> p c t i", i=4),
            )

        b_k_bytes = chain.tile([P, H], U8, name="b_k_bytes", offset=5 * H)
        b_x_bytes = chain.tile([P, S], U8, name="b_x_bytes", offset=7 * H)
        b_staged = keep.tile([P, H + S], U8, name="b_staged")
        b_sums = coded_product("b", l_k2, l_two, nc.sync, b_k_bytes, b_x_bytes, b_staged, H, TILES)

        ex = [chain.tile([P, EX_WINDOW], F32, name="ex%d" % t, offset=(21 - 8 * t) * H) for t in range(2)]
        ex = ex + [keep.tile([P, EX_WINDOW], F32, name="ex%d" % t) for t in range(2, TILES)]
        for t in range(TILES):
            nc.scalar.activation(ex[t][:, 0:S], a_sums[t][:], ACT.Exp, scale=0.03125)
        first = keep.tile([P, TILES, S], F32, name="first")
        both = keep.tile([P, TILES, S], F32, name="both")
        for t in range(TILES):
            nc.scalar.activation(first[:, t, :], ex[t][:].indirect(l_n1[:]), ACT.Copy)
        for t in range(TILES):
            nc.vector.tensor_tensor(both[:, t, :], ex[t][:].indirect(l_n2[:]), first[:, t, :], ALU.add)

        b = [keep.tile([P, B_WINDOW], F32, name="b%d" % t) for t in range(TILES)]
        members = keep.tile([P, TILES, S, 2], F32, name="members")
        low = keep.tile([P, TILES, S], F32, name="low")
        high = keep.tile([P, TILES, S], F32, name="high")
        rise = keep.tile([P, TILES, S], F32, name="rise")
        logs = first
        gate = both
        gn_twice = keep.tile([P, PACK], F32, name="gn_twice")
        nc.vector.tensor_scalar(gn_twice[:], gn_t[:], 2.0, None, ALU.mult)
        z2_rows = keep.tile([P, TILES, S], BF16, name="z2_rows")
        halves = (slice(0, HALF), slice(HALF, S))
        pairs = ((0, 1), (2, 3))

        def move(on_scalar, dst, src):
            if on_scalar:
                nc.scalar.activation(dst, src, ACT.Copy)
            else:
                nc.vector.tensor_copy(dst, src)

        def fetch_members(half, t, on_scalar):
            entries = l_n3[:, half * 32 : (half + 1) * 32]
            move(on_scalar, members[:, t, halves[half], :].rearrange("p j e -> p (j e)"), b[t][:].indirect(entries))

        def compare_members(half, pair):
            cols = halves[half]
            ts = slice(pair[0], pair[1] + 1)
            nc.vector.tensor_tensor(high[:, ts, cols], members[:, ts, cols, 0], members[:, ts, cols, 1], ALU.max)
            nc.vector.tensor_tensor(low[:, ts, cols], members[:, ts, cols, 0], members[:, ts, cols, 1], ALU.min)
            nc.scalar.activation(gate[:, ts, cols], high[:, ts, cols], ACT.Sigmoid)
            for t in pair:
                nc.vector.tensor_tensor(rise[:, t, cols], b[t][:, cols], low[:, t, cols], ALU.subtract)

        def gated(half, pair):
            cols = halves[half]
            for t in pair:
                nc.vector.scalar_tensor_tensor(
                    z2_rows[:, t, cols], rise[:, t, cols], gm_t[:, t : t + 1], gate[:, t, cols], ALU.mult, ALU.mult
                )

        for t in range(TILES):
            nc.scalar.activation(b[t][:, 0:S], b_sums[t][:], ACT.Copy, scale=0.0625)
        fetch_members(0, 0, True)
        nc.scalar.activation(logs[:], both[:], ACT.Ln)
        fetch_members(0, 1, False)
        fetch_members(0, 2, False)

        w1_codes, w1_scales = quantize("w1", w1_grouped)
        w2_grouped = chain.tile([P, N, PACK], BF16, name="w2_grouped", offset=13 * H, align_bytes=64)
        dst, src = weave_views(w2_grouped, w2_raw)
        nc.vector.tensor_copy(dst, src)
        w2_codes, w2_scales = quantize("w2", w2_grouped)
        logit = keep.tile([P, TILES, S], F32, name="logit")
        share = keep.tile([P, TILES, S], F32, name="share")
        for t in range(TILES):
            nc.vector.scalar_tensor_tensor(logit[:, t, :], a_sums[t][:], 0.03125, logs[:, t, :], ALU.mult, ALU.subtract)
        for t in range(TILES):
            nc.scalar.activation(share[:, t, :], logit[:, t, :], ACT.Sigmoid)
        z_grouped = keep.tile([P, S, PACK], BF16, name="z_grouped", align_bytes=64)
        dst, src = weave_views(z_grouped, share)
        gains = gn_twice[:].unsqueeze(1).unsqueeze(3).to_broadcast([P, S // 4, PACK, 4])
        nc.vector.tensor_tensor(dst, src, gains, ALU.mult)
        z_codes, z_scales = quantize("z", z_grouped)

        z2_grouped = keep.tile([P, S, PACK], BF16, name="z2_grouped", align_bytes=64)
        z2_codes = keep.tile([P, S], U32, name="z2_codes", align_bytes=64)
        z2_scales = keep.tile([P, S], U8, name="z2_scales", align_bytes=64)

        def quantize_z2(half):
            cols = halves[half]
            nc.vector.quantize_mx(
                out=z2_codes[:, cols].bitcast(FP8X4),
                scales=z2_scales[:, cols],
                in_=z2_grouped[:, cols, :].rearrange("p w j -> p (w j)"),
            )

        compare_members(0, pairs[0])
        fetch_members(0, 3, True)
        compare_members(0, pairs[1])
        gated(0, pairs[0])
        fetch_members(1, 0, True)
        fetch_members(1, 1, True)
        compare_members(1, pairs[0])
        gated(0, pairs[1])
        dst, src = weave_views(z2_grouped, z2_rows, halves[0])
        nc.scalar.copy(dst, src)
        quantize_z2(0)
        fetch_members(1, 2, True)
        fetch_members(1, 3, True)
        compare_members(1, pairs[1])
        gated(1, pairs[0])
        gated(1, pairs[1])
        dst, src = weave_views(z2_grouped, z2_rows, halves[1])
        nc.vector.tensor_copy(dst, src)
        quantize_z2(1)

        h = [keep.tile([P, S], F32, name="h%d" % m) for m in range(TILES)]
        for half in range(2):
            cols = halves[half]
            h_sums = [
                psum.tile([P, HALF], F32, name="h_sum%d_%d" % (half, m), tag="bank%d" % ((1 - half) * TILES + m))
                for m in range(TILES)
            ]
            for step, (w_codes, w_scales, v_codes, v_scales) in enumerate(
                ((w1_codes, w1_scales, z_codes, z_scales), (w2_codes, w2_scales, z2_codes, z2_scales))
            ):
                for m in range(TILES):
                    rows = slice(m * P, (m + 1) * P)
                    nc.tensor.matmul_mx(
                        out=h_sums[m][:],
                        lhsT=w_codes[:, rows].bitcast(FP8X4),
                        lhsT_scale=w_scales[:, rows],
                        rhs=v_codes[:, cols].bitcast(FP8X4),
                        rhs_scale=v_scales[:, cols],
                        start=(step == 0),
                        stop=(step == 1),
                    )
            for m in range(TILES):
                move(half == 0 or m != 1, h[m][:, cols], h_sums[m][:])

        pa = [keep.tile([P, U], F32, name="pa%d" % m) for m in range(TILES)]
        old = [keep.tile([P, U], F32, name="old%d" % m) for m in range(TILES)]
        ra = [keep.tile([P, U], F32, name="ra%d" % m) for m in range(TILES)]
        for m in range(TILES):
            move(m % 2 == 0, pa[m][:], h[m][:].indirect(l_n5[:]))
            move(m != 1, old[m][:], h[m][:].indirect(l_n4[:]))
        for m in range(TILES):
            nc.vector.scalar_tensor_tensor(ra[m][:], old[m][:], 0.5, pa[m][:], ALU.mult, ALU.max)
        for m in range(TILES):
            move(m % 2 == 0, h[m][:].indirect(l_n4[:]), ra[m][:])
            nc.sync.dma_start(out[m * P : (m + 1) * P, :], h[m][:])
